import numpy as np
import ml_dtypes


def mxq(x, axis, fmt="e4m3"):
    dtype, down = {"e4m3": (ml_dtypes.float8_e4m3fn, 7), "e5m2": (ml_dtypes.float8_e5m2, 14)}[fmt]
    v = np.moveaxis(np.asarray(x, np.float32).astype(ml_dtypes.bfloat16).astype(np.float64), axis, -1)
    blocks = v.reshape(v.shape[:-1] + (-1, 32))
    amax = np.abs(blocks).max(-1, keepdims=True)
    byte = np.maximum(np.where(amax > 0, np.frexp(amax)[1] - 1 + 127, 0) - down, 1)
    scale = np.exp2(byte - 127.0)
    codes = (blocks / scale).astype(np.float32).astype(dtype).astype(np.float64)
    return np.moveaxis((codes * scale).reshape(v.shape), -1, axis)


WIDE = False


def mx_kscale(k):
    if not WIDE:
        return np.ones(k)
    levels = np.array([10, -10, 5, -5, 0])
    if k % 512:
        return np.exp2(np.random.permutation(np.resize(levels, k // 32))).repeat(32)
    a = np.empty((k // 512, 16))
    for p in range(k // 512):
        a[p, :8] = np.random.permutation(np.resize(levels, 8))
        for g in range(8):
            far = levels[np.abs(levels - a[p, g]) >= 10]
            a[p, g + 8] = far[np.random.randint(len(far))]
    return np.exp2(a.ravel()).repeat(32)


def f64(x):
    return np.asarray(x).astype(np.float64)


def striped8(idx):
    return np.asarray(idx).reshape(8, -1, 16).transpose(0, 2, 1).reshape(128, -1).astype(np.uint16)


def unstriped8(offs):
    return offs.reshape(8, 16, -1).transpose(0, 2, 1).reshape(8, -1).astype(np.int64)


def pick8(x, idx, run):
    r = np.arange(len(x))
    return x[r[:, None], idx[r % (8 * run) // run]]


E2M1 = np.array([0.0, 0.5, 1.0, 1.5, 2.0, 3.0, 4.0, 6.0, -0.0, -0.5, -1.0, -1.5, -2.0, -3.0, -4.0, -6.0])


def pack_weight(w, fmt):
    k, n = w.shape
    w = f64(np.asarray(w, np.float32).astype(ml_dtypes.bfloat16)).reshape(k // 32, 32, n)
    amax = np.abs(w).max(1)
    if fmt == "e4m3":
        byte = np.frexp(amax)[1] - 1 + 127 - 7
    else:
        mant, ex = np.frexp(amax / 6.0)
        byte = np.where(mant > 0.5, ex, ex - 1) + 127
    byte = np.clip(np.where(amax > 0, byte, 1), 1, 254)
    scaled = (w * np.exp2(127.0 - byte)[:, None, :]).reshape(k, n).astype(np.float32)
    by_word = np.ascontiguousarray(scaled.reshape(k // 512, 128, 4, n).transpose(0, 1, 3, 2))
    if fmt == "e4m3":
        words = by_word.astype(ml_dtypes.float8_e4m3fn).view(np.uint8)
    else:
        c = by_word.astype(ml_dtypes.float4_e2m1fn).view(np.uint8) & 0xF
        words = (c[..., 0::2] | (c[..., 1::2] << 4)).reshape(k // 512, 128, 2 * n)
    return np.ascontiguousarray(words), np.ascontiguousarray(byte.astype(np.uint8).reshape(k // 512, 16, n))


def unpack_weight(words, scales, fmt):
    g, _, n = scales.shape
    words = np.ascontiguousarray(words).reshape(g, 128, n, -1)
    if fmt == "e4m3":
        vals = words.view(ml_dtypes.float8_e4m3fn).astype(np.float64)
    else:
        nib = np.empty((g, 128, n, 4), np.uint8)
        nib[..., 0::2] = words & 0xF
        nib[..., 1::2] = words >> 4
        vals = E2M1[nib]
    vals = vals * np.repeat(np.exp2(scales.astype(np.float64) - 127.0), 8, axis=1)[..., None]
    return vals.transpose(0, 1, 3, 2).reshape(g * 512, n)


D, K, T, U, I, Q = 512, 512, 1024, 1024, 512, 128


def setup_inputs():
    n = np.random.standard_normal
    idx = np.stack([np.random.permutation(T)[:I] for _ in range(8)])
    idx2 = np.stack([np.random.permutation(U)[:I] for _ in range(8)])
    idx3 = np.stack([np.random.permutation(U)[:I] for _ in range(8)])
    fd = mx_kscale(D)
    fk = mx_kscale(K)
    wqp = pack_weight(n((D, K)) * 1.0 / np.sqrt(D) * fd[:, None] * fk, "e4m3")
    keysp = pack_weight(n((K, T)) * 1.0 / np.sqrt(K) / fk[:, None], "e4m3")
    notesp = pack_weight(n((D, U)) * 1.0 / np.sqrt(D) * fd[:, None], "e2m1")
    return {
        "states": (n((D, Q)) * 0.95 / fd[:, None]).astype(np.float32),
        "wq_words": wqp[0],
        "wq_scales": wqp[1],
        "keys_words": keysp[0],
        "keys_scales": keysp[1],
        "notes_words": notesp[0],
        "notes_scales": notesp[1],
        "tau": (np.random.uniform(0.5, 1.5, (Q, 1))).astype(np.float32),
        "offs": striped8(idx),
        "offs2": striped8(idx2),
        "offs3": striped8(idx3),
    }


def reference(states, wq_words, wq_scales, keys_words, keys_scales, notes_words, notes_scales, tau, offs, offs2, offs3):
    idx = unstriped8(offs)
    idx2 = unstriped8(offs2)
    idx3 = unstriped8(offs3)
    wqu = unpack_weight(wq_words, wq_scales, "e4m3")
    keysu = unpack_weight(keys_words, keys_scales, "e4m3")
    notesu = unpack_weight(notes_words, notes_scales, "e2m1")
    statesq = mxq(f64(states), 0, "e4m3")
    qv = wqu.T @ statesq
    qvq = mxq(qv, 0, "e4m3")
    a = qvq.T @ keysu
    b = statesq.T @ notesu
    ta = np.max(a, axis=1, keepdims=True)
    bt = ta * f64(tau)
    e1 = np.exp(pick8(a, idx, 16) * f64(tau) - bt)
    f1 = np.zeros((Q, U))
    f1[np.arange(Q)[:, None], idx2[np.arange(Q) % 128 // 16]] = e1
    cc = b + f1 * 4.0
    y = pick8(cc, idx3, 16) - e1
    return y

@@ -1,0 +1,194 @@
+from contextlib import ExitStack
+
+import concourse.mybir as mybir
+
+FLOPS = 335544320
+
+F32 = mybir.dt.float32
+BF16 = mybir.dt.bfloat16
+I32 = mybir.dt.int32
+U32 = mybir.dt.uint32
+U16 = mybir.dt.uint16
+U8 = mybir.dt.uint8
+FP8X4 = mybir.dt.float8_e4m3fn_x4
+FP4X4 = mybir.dt.float4_e2m1fn_x4
+ALU = mybir.AluOpType
+ACT = mybir.ActivationFunctionType
+
+P = 128
+PACK = 4
+Q = 128
+K = 512
+T = 1024
+U = 1024
+SLOTS = 512
+LIST_COLS = SLOTS // 16
+HALF = SLOTS // 2
+HALF_COLS = LIST_COLS // 2
+A_CHUNK = 256
+BANK = 512
+
+
+def load_scale_rows(queue, plane, rows):
+    for quad in range(4):
+        queue.dma_start(
+            out=plane[32 * quad : 32 * quad + 4, :].bitcast(I32),
+            in_=rows[0, 4 * quad : 4 * quad + 4, :].bitcast(I32),
+        )
+
+
+def tile_attend_temperedvotes_madeside_kernel(
+    tc, states, wq_words, wq_scales, keys_words, keys_scales, notes_words, notes_scales, tau, offs, offs2, offs3, out
+):
+    nc = tc.nc
+    with ExitStack() as ctx:
+        sb = ctx.enter_context(tc.tile_pool(name="sb", bufs=1))
+        ps = ctx.enter_context(tc.psum_pool(name="ps", bufs=1))
+
+        wq_plane = sb.tile([P, K], U8, name="wq_plane", align_bytes=64)
+        keys_plane = sb.tile([P, T], U8, name="keys_plane", align_bytes=64)
+        notes_plane = sb.tile([P, U], U8, name="notes_plane", align_bytes=64)
+        votes = sb.tile([P, U], F32, name="votes", align_bytes=64)
+        nc.vector.memset(wq_plane[:].bitcast(I32), 0)
+        nc.vector.memset(keys_plane[:].bitcast(I32), 0)
+        nc.vector.memset(notes_plane[:].bitcast(I32), 0)
+        nc.vector.memset(votes[:], 0.0)
+
+        states_raw = sb.tile([P, PACK, Q], F32, name="states_raw", align_bytes=64)
+        wq_raw = sb.tile([P, K], U32, name="wq_raw", align_bytes=64)
+        keys_codes = sb.tile([P, T], U32, name="keys_codes", align_bytes=64)
+        notes_codes = sb.tile([P, 2 * U], U8, name="notes_codes", align_bytes=64)
+        tau_col = sb.tile([P, 1], F32, name="tau_col")
+        token_list = sb.tile([P, LIST_COLS], U16, name="token_list")
+        vote_list = sb.tile([P, LIST_COLS], U16, name="vote_list")
+        read_list = sb.tile([P, LIST_COLS], U16, name="read_list")
+
+        nc.sync.dma_start(out=states_raw[:], in_=states.rearrange("(p j) q -> p j q", j=PACK))
+        load_scale_rows(nc.scalar, wq_plane, wq_scales)
+        nc.sync.dma_start(out=wq_raw[:].bitcast(I32), in_=wq_words[0].rearrange("p n t -> p (n t)").bitcast(I32))
+        nc.sync.dma_start(out=keys_codes[:].bitcast(I32), in_=keys_words[0].rearrange("p n t -> p (n t)").bitcast(I32))
+        load_scale_rows(nc.sync, keys_plane, keys_scales)
+        nc.sync.dma_start(out=tau_col[:], in_=tau)
+        nc.sync.dma_start(token_list[:], offs)
+        nc.sync.dma_start(out=notes_codes[:].bitcast(I32), in_=notes_words[0].bitcast(I32))
+        load_scale_rows(nc.sync, notes_plane, notes_scales)
+        nc.sync.dma_start(vote_list[:], offs2)
+        nc.sync.dma_start(read_list[:], offs3)
+
+        states_bf = sb.tile([P, Q, PACK], BF16, name="states_bf", align_bytes=64)
+        nc.vector.tensor_copy(
+            out=states_bf[:].rearrange("p (c i) t -> p c t i", i=4),
+            in_=states_raw[:].rearrange("p t (c i) -> p c t i", i=4),
+        )
+        wq_dealt_plane = sb.tile([P, PACK, P], U8, name="wq_dealt_plane", align_bytes=64)
+        nc.vector.tensor_copy(
+            out=wq_dealt_plane[:].rearrange("p t m -> p m t"),
+            in_=wq_plane[:].rearrange("p (m t) -> p m t", t=PACK),
+        )
+        states_codes = sb.tile([P, Q], U32, name="states_codes", align_bytes=64)
+        states_plane = sb.tile([P, Q], U8, name="states_plane", align_bytes=64)
+        nc.vector.quantize_mx(
+            out=states_codes[:].bitcast(FP8X4), scales=states_plane[:], in_=states_bf[:].rearrange("p q t -> p (q t)")
+        )
+        wq_dealt = sb.tile([P, PACK, P], U32, name="wq_dealt", align_bytes=64)
+        nc.scalar.copy(
+            out=wq_dealt[:].rearrange("p t m -> p m t"),
+            in_=wq_raw[:].rearrange("p (m t) -> p m t", t=PACK),
+        )
+
+        qv_bank = ps.tile([P, PACK, Q], F32, name="qv_bank")
+        for t in range(PACK):
+            nc.tensor.matmul_mx(
+                out=qv_bank[:, t, :],
+                lhsT=wq_dealt[:, t, :].bitcast(FP8X4),
+                lhsT_scale=wq_dealt_plane[:, t, :],
+                rhs=states_codes[:].bitcast(FP8X4),
+                rhs_scale=states_plane[:],
+                start=True,
+                stop=True,
+            )
+        qv_bf = sb.tile([P, Q, PACK], BF16, name="qv_bf", align_bytes=64)
+        nc.scalar.copy(out=qv_bf[:], in_=qv_bank[:].rearrange("p t q -> p q t"))
+        qv_codes = sb.tile([P, Q], U32, name="qv_codes", align_bytes=64)
+        qv_plane = sb.tile([P, Q], U8, name="qv_plane", align_bytes=64)
+        nc.vector.quantize_mx(
+            out=qv_codes[:].bitcast(FP8X4), scales=qv_plane[:], in_=qv_bf[:].rearrange("p q t -> p (q t)")
+        )
+
+        neg_tau = sb.tile([P, 1], F32, name="neg_tau")
+        nc.vector.tensor_scalar(out=neg_tau[:], in0=tau_col[:], scalar1=-1.0, scalar2=None, op0=ALU.mult)
+
+        scores = sb.tile([P, T], F32, name="scores", align_bytes=64)
+        running = []
+        for c in range(T // A_CHUNK):
+            cols = slice(c * A_CHUNK, (c + 1) * A_CHUNK)
+            a_bank = ps.tile([P, A_CHUNK], F32, name="a_bank%d" % c)
+            nc.tensor.matmul_mx(
+                out=a_bank[:],
+                lhsT=qv_codes[:].bitcast(FP8X4),
+                lhsT_scale=qv_plane[:],
+                rhs=keys_codes[:, cols].bitcast(FP8X4),
+                rhs_scale=keys_plane[:, cols],
+                start=True,
+                stop=True,
+            )
+            largest = sb.tile([P, 1], F32, name="largest%d" % c)
+            nc.vector.tensor_scalar(
+                out=scores[:, cols],
+                in0=a_bank[:],
+                scalar1=1.0,
+                scalar2=running[c - 2][:] if c >= 2 else None,
+                op0=ALU.mult,
+                op1=ALU.max,
+                accum_out=largest[:],
+            )
+            running.append(largest)
+        neg_bt = sb.tile([P, 1], F32, name="neg_bt")
+        nc.vector.tensor_scalar(
+            out=neg_bt[:], in0=running[-2][:], scalar1=running[-1][:], scalar2=neg_tau[:], op0=ALU.max, op1=ALU.mult
+        )
+
+        b_banks = []
+        for h in range(U // BANK):
+            b_bank = ps.tile([P, BANK], F32, name="b_bank%d" % h)
+            nc.tensor.matmul_mx(
+                out=b_bank[:],
+                lhsT=states_codes[:].bitcast(FP8X4),
+                lhsT_scale=states_plane[:],
+                rhs=notes_codes[:, 2 * BANK * h : 2 * BANK * (h + 1)].bitcast(FP4X4),
+                rhs_scale=notes_plane[:, BANK * h : BANK * (h + 1)],
+                start=True,
+                stop=True,
+            )
+            b_banks.append(b_bank)
+
+        e1 = sb.tile([P, SLOTS], F32, name="e1", align_bytes=64)
+        for h in range(2):
+            slots = slice(h * HALF, (h + 1) * HALF)
+            list_cols = slice(h * HALF_COLS, (h + 1) * HALF_COLS)
+            nc.scalar.activation(
+                out=e1[:, slots],
+                in_=scores[:].indirect(token_list[:, list_cols]),
+                func=ACT.Exp,
+                bias=neg_bt[:],
+                scale=tau_col[:],
+            )
+            nc.vector.tensor_copy(out=votes[:].indirect(vote_list[:, list_cols]), in_=e1[:, slots])
+
+        cc = sb.tile([P, U], F32, name="cc", align_bytes=64)
+        for h in range(U // BANK):
+            cols = slice(h * BANK, (h + 1) * BANK)
+            nc.vector.scalar_tensor_tensor(
+                out=cc[:, cols], in0=votes[:, cols], scalar=4.0, in1=b_banks[h][:], op0=ALU.mult, op1=ALU.add
+            )
+
+        low = sb.tile([P, HALF], F32, name="low", align_bytes=64)
+        picked = sb.tile([P, HALF], F32, name="picked", align_bytes=64)
+        high = sb.tile([P, HALF], F32, name="high", align_bytes=64)
+        nc.vector.tensor_tensor(
+            out=low[:], in0=cc[:].indirect(read_list[:, :HALF_COLS]), in1=e1[:, :HALF], op=ALU.subtract
+        )
+        nc.scalar.activation(out=picked[:], in_=cc[:].indirect(read_list[:, HALF_COLS:]), func=ACT.Copy)
+        nc.sync.dma_start(out=out[:, :HALF], in_=low[:])
+        nc.vector.tensor_tensor(out=high[:], in0=picked[:], in1=e1[:, HALF:], op=ALU.subtract)
+        nc.sync.dma_start(out=out[:, HALF:], in_=high[:])

@@ -29,9 +29,9 @@ A_CHUNK = 256
 BANK = 512
 
 
-def load_scale_rows(queue, plane, rows):
+def load_scale_rows(queues, plane, rows):
     for quad in range(4):
-        queue.dma_start(
+        queues[quad % len(queues)].dma_start(
             out=plane[32 * quad : 32 * quad + 4, :].bitcast(I32),
             in_=rows[0, 4 * quad : 4 * quad + 4, :].bitcast(I32),
         )
@@ -64,14 +64,14 @@ def tile_attend_temperedvotes_madeside_kernel(
         read_list = sb.tile([P, LIST_COLS], U16, name="read_list")
 
         nc.sync.dma_start(out=states_raw[:], in_=states.rearrange("(p j) q -> p j q", j=PACK))
-        load_scale_rows(nc.scalar, wq_plane, wq_scales)
+        load_scale_rows((nc.scalar, nc.sync), wq_plane, wq_scales)
+        nc.scalar.dma_start(out=tau_col[:], in_=tau)
         nc.sync.dma_start(out=wq_raw[:].bitcast(I32), in_=wq_words[0].rearrange("p n t -> p (n t)").bitcast(I32))
         nc.sync.dma_start(out=keys_codes[:].bitcast(I32), in_=keys_words[0].rearrange("p n t -> p (n t)").bitcast(I32))
-        load_scale_rows(nc.sync, keys_plane, keys_scales)
-        nc.sync.dma_start(out=tau_col[:], in_=tau)
+        load_scale_rows((nc.sync,), keys_plane, keys_scales)
         nc.sync.dma_start(token_list[:], offs)
         nc.sync.dma_start(out=notes_codes[:].bitcast(I32), in_=notes_words[0].bitcast(I32))
-        load_scale_rows(nc.sync, notes_plane, notes_scales)
+        load_scale_rows((nc.sync,), notes_plane, notes_scales)
         nc.sync.dma_start(vote_list[:], offs2)
         nc.sync.dma_start(read_list[:], offs3)
 
@@ -81,34 +81,44 @@ def tile_attend_temperedvotes_madeside_kernel(
             in_=states_raw[:].rearrange("p t (c i) -> p c t i", i=4),
         )
         wq_dealt_plane = sb.tile([P, PACK, P], U8, name="wq_dealt_plane", align_bytes=64)
-        nc.vector.tensor_copy(
-            out=wq_dealt_plane[:].rearrange("p t m -> p m t"),
-            in_=wq_plane[:].rearrange("p (m t) -> p m t", t=PACK),
-        )
+
+        def deal_scales(pair):
+            places = slice(2 * pair, 2 * pair + 2)
+            nc.vector.tensor_copy(
+                out=wq_dealt_plane[:, places, :].rearrange("p t m -> p m t"),
+                in_=wq_plane[:].rearrange("p (m t) -> p m t", t=PACK)[:, :, places],
+            )
+
+        deal_scales(0)
         states_codes = sb.tile([P, Q], U32, name="states_codes", align_bytes=64)
         states_plane = sb.tile([P, Q], U8, name="states_plane", align_bytes=64)
         nc.vector.quantize_mx(
             out=states_codes[:].bitcast(FP8X4), scales=states_plane[:], in_=states_bf[:].rearrange("p q t -> p (q t)")
         )
+        deal_scales(1)
         wq_dealt = sb.tile([P, PACK, P], U32, name="wq_dealt", align_bytes=64)
-        nc.scalar.copy(
-            out=wq_dealt[:].rearrange("p t m -> p m t"),
-            in_=wq_raw[:].rearrange("p (m t) -> p m t", t=PACK),
-        )
-
-        qv_bank = ps.tile([P, PACK, Q], F32, name="qv_bank")
-        for t in range(PACK):
-            nc.tensor.matmul_mx(
-                out=qv_bank[:, t, :],
-                lhsT=wq_dealt[:, t, :].bitcast(FP8X4),
-                lhsT_scale=wq_dealt_plane[:, t, :],
-                rhs=states_codes[:].bitcast(FP8X4),
-                rhs_scale=states_plane[:],
-                start=True,
-                stop=True,
+        for pair in range(2):
+            places = slice(2 * pair, 2 * pair + 2)
+            nc.scalar.copy(
+                out=wq_dealt[:, places, :].rearrange("p t m -> p m t"),
+                in_=wq_raw[:].rearrange("p (m t) -> p m t", t=PACK)[:, :, places],
             )
+
         qv_bf = sb.tile([P, Q, PACK], BF16, name="qv_bf", align_bytes=64)
-        nc.scalar.copy(out=qv_bf[:], in_=qv_bank[:].rearrange("p t q -> p q t"))
+        for pair, copy in enumerate((nc.vector.tensor_copy, nc.scalar.copy)):
+            qv_bank = ps.tile([P, 2, Q], F32, name="qv_bank%d" % pair)
+            for e in range(2):
+                t = 2 * pair + e
+                nc.tensor.matmul_mx(
+                    out=qv_bank[:, e, :],
+                    lhsT=wq_dealt[:, t, :].bitcast(FP8X4),
+                    lhsT_scale=wq_dealt_plane[:, t, :],
+                    rhs=states_codes[:].bitcast(FP8X4),
+                    rhs_scale=states_plane[:],
+                    start=True,
+                    stop=True,
+                )
+            copy(out=qv_bf[:, :, 2 * pair : 2 * pair + 2], in_=qv_bank[:].rearrange("p e q -> p q e"))
         qv_codes = sb.tile([P, Q], U32, name="qv_codes", align_bytes=64)
         qv_plane = sb.tile([P, Q], U8, name="qv_plane", align_bytes=64)
         nc.vector.quantize_mx(

@@ -27,6 +27,7 @@ HALF = SLOTS // 2
 HALF_COLS = LIST_COLS // 2
 A_CHUNK = 256
 BANK = 512
+SIDE = 256
 
 
 def load_scale_rows(queues, plane, rows):
@@ -53,6 +54,8 @@ def tile_attend_temperedvotes_madeside_kernel(
         nc.vector.memset(keys_plane[:].bitcast(I32), 0)
         nc.vector.memset(notes_plane[:].bitcast(I32), 0)
         nc.vector.memset(votes[:], 0.0)
+        fours = sb.tile([P, HALF], F32, name="fours", align_bytes=64)
+        nc.vector.memset(fours[:], 4.0)
 
         states_raw = sb.tile([P, PACK, Q], F32, name="states_raw", align_bytes=64)
         wq_raw = sb.tile([P, K], U32, name="wq_raw", align_bytes=64)
@@ -65,7 +68,7 @@ def tile_attend_temperedvotes_madeside_kernel(
 
         nc.sync.dma_start(out=states_raw[:], in_=states.rearrange("(p j) q -> p j q", j=PACK))
         load_scale_rows((nc.scalar, nc.sync), wq_plane, wq_scales)
-        nc.scalar.dma_start(out=tau_col[:], in_=tau)
+        nc.sync.dma_start(out=tau_col[:], in_=tau)
         nc.sync.dma_start(out=wq_raw[:].bitcast(I32), in_=wq_words[0].rearrange("p n t -> p (n t)").bitcast(I32))
         nc.sync.dma_start(out=keys_codes[:].bitcast(I32), in_=keys_words[0].rearrange("p n t -> p (n t)").bitcast(I32))
         load_scale_rows((nc.sync,), keys_plane, keys_scales)
@@ -183,14 +186,15 @@ def tile_attend_temperedvotes_madeside_kernel(
                 bias=neg_bt[:],
                 scale=tau_col[:],
             )
-            nc.vector.tensor_copy(out=votes[:].indirect(vote_list[:, list_cols]), in_=e1[:, slots])
+            nc.vector.tensor_tensor(out=votes[:].indirect(vote_list[:, list_cols]), in0=e1[:, slots], in1=fours[:], op=ALU.mult)
 
+        b_side = sb.tile([P, SIDE], F32, name="b_side", align_bytes=64)
+        nc.scalar.copy(out=b_side[:], in_=b_banks[1][:, BANK - SIDE :])
         cc = sb.tile([P, U], F32, name="cc", align_bytes=64)
-        for h in range(U // BANK):
-            cols = slice(h * BANK, (h + 1) * BANK)
-            nc.vector.scalar_tensor_tensor(
-                out=cc[:, cols], in0=votes[:, cols], scalar=4.0, in1=b_banks[h][:], op0=ALU.mult, op1=ALU.add
-            )
+        split = U - SIDE
+        nc.gpsimd.tensor_tensor(out=cc[:, split:], in0=votes[:, split:], in1=b_side[:], op=ALU.add)
+        nc.vector.tensor_tensor(out=cc[:, :BANK], in0=votes[:, :BANK], in1=b_banks[0][:], op=ALU.add)
+        nc.vector.tensor_tensor(out=cc[:, BANK:split], in0=votes[:, BANK:split], in1=b_banks[1][:, : split - BANK], op=ALU.add)
 
         low = sb.tile([P, HALF], F32, name="low", align_bytes=64)
         picked = sb.tile([P, HALF], F32, name="picked", align_bytes=64)

from contextlib import ExitStack

import concourse.mybir as mybir

FLOPS = 335544320

F32 = mybir.dt.float32
BF16 = mybir.dt.bfloat16
I32 = mybir.dt.int32
U32 = mybir.dt.uint32
U16 = mybir.dt.uint16
U8 = mybir.dt.uint8
FP8X4 = mybir.dt.float8_e4m3fn_x4
FP4X4 = mybir.dt.float4_e2m1fn_x4
ALU = mybir.AluOpType
ACT = mybir.ActivationFunctionType

P = 128
PACK = 4
Q = 128
K = 512
T = 1024
U = 1024
SLOTS = 512
LIST_COLS = SLOTS // 16
HALF = SLOTS // 2
HALF_COLS = LIST_COLS // 2
A_CHUNK = 256
BANK = 512
SIDE = 256


def load_scale_rows(queues, plane, rows):
    for quad in range(4):
        queues[quad % len(queues)].dma_start(
            out=plane[32 * quad : 32 * quad + 4, :].bitcast(I32),
            in_=rows[0, 4 * quad : 4 * quad + 4, :].bitcast(I32),
        )


def tile_attend_temperedvotes_madeside_kernel(
    tc, states, wq_words, wq_scales, keys_words, keys_scales, notes_words, notes_scales, tau, offs, offs2, offs3, out
):
    nc = tc.nc
    with ExitStack() as ctx:
        sb = ctx.enter_context(tc.tile_pool(name="sb", bufs=1))
        ps = ctx.enter_context(tc.psum_pool(name="ps", bufs=1))

        wq_plane = sb.tile([P, K], U8, name="wq_plane", align_bytes=64)
        keys_plane = sb.tile([P, T], U8, name="keys_plane", align_bytes=64)
        notes_plane = sb.tile([P, U], U8, name="notes_plane", align_bytes=64)
        votes = sb.tile([P, U], F32, name="votes", align_bytes=64)
        nc.vector.memset(wq_plane[:].bitcast(I32), 0)
        nc.vector.memset(keys_plane[:].bitcast(I32), 0)
        nc.vector.memset(notes_plane[:].bitcast(I32), 0)
        nc.vector.memset(votes[:], 0.0)
        fours = sb.tile([P, HALF], F32, name="fours", align_bytes=64)
        nc.vector.memset(fours[:], 4.0)

        states_raw = sb.tile([P, PACK, Q], F32, name="states_raw", align_bytes=64)
        wq_raw = sb.tile([P, K], U32, name="wq_raw", align_bytes=64)
        keys_codes = sb.tile([P, T], U32, name="keys_codes", align_bytes=64)
        notes_codes = sb.tile([P, 2 * U], U8, name="notes_codes", align_bytes=64)
        tau_col = sb.tile([P, 1], F32, name="tau_col")
        token_list = sb.tile([P, LIST_COLS], U16, name="token_list")
        vote_list = sb.tile([P, LIST_COLS], U16, name="vote_list")
        read_list = sb.tile([P, LIST_COLS], U16, name="read_list")

        nc.sync.dma_start(out=states_raw[:], in_=states.rearrange("(p j) q -> p j q", j=PACK))
        load_scale_rows((nc.scalar, nc.sync), wq_plane, wq_scales)
        nc.sync.dma_start(out=tau_col[:], in_=tau)
        nc.sync.dma_start(out=wq_raw[:].bitcast(I32), in_=wq_words[0].rearrange("p n t -> p (n t)").bitcast(I32))
        nc.sync.dma_start(out=keys_codes[:].bitcast(I32), in_=keys_words[0].rearrange("p n t -> p (n t)").bitcast(I32))
        load_scale_rows((nc.sync,), keys_plane, keys_scales)
        nc.sync.dma_start(token_list[:], offs)
        nc.sync.dma_start(out=notes_codes[:].bitcast(I32), in_=notes_words[0].bitcast(I32))
        load_scale_rows((nc.sync,), notes_plane, notes_scales)
        nc.sync.dma_start(vote_list[:], offs2)
        nc.sync.dma_start(read_list[:], offs3)

        states_bf = sb.tile([P, Q, PACK], BF16, name="states_bf", align_bytes=64)
        nc.vector.tensor_copy(
            out=states_bf[:].rearrange("p (c i) t -> p c t i", i=4),
            in_=states_raw[:].rearrange("p t (c i) -> p c t i", i=4),
        )
        wq_dealt_plane = sb.tile([P, PACK, P], U8, name="wq_dealt_plane", align_bytes=64)

        def deal_scales(pair):
            places = slice(2 * pair, 2 * pair + 2)
            nc.vector.tensor_copy(
                out=wq_dealt_plane[:, places, :].rearrange("p t m -> p m t"),
                in_=wq_plane[:].rearrange("p (m t) -> p m t", t=PACK)[:, :, places],
            )

        deal_scales(0)
        states_codes = sb.tile([P, Q], U32, name="states_codes", align_bytes=64)
        states_plane = sb.tile([P, Q], U8, name="states_plane", align_bytes=64)
        nc.vector.quantize_mx(
            out=states_codes[:].bitcast(FP8X4), scales=states_plane[:], in_=states_bf[:].rearrange("p q t -> p (q t)")
        )
        deal_scales(1)
        wq_dealt = sb.tile([P, PACK, P], U32, name="wq_dealt", align_bytes=64)
        for pair in range(2):
            places = slice(2 * pair, 2 * pair + 2)
            nc.scalar.copy(
                out=wq_dealt[:, places, :].rearrange("p t m -> p m t"),
                in_=wq_raw[:].rearrange("p (m t) -> p m t", t=PACK)[:, :, places],
            )

        qv_bf = sb.tile([P, Q, PACK], BF16, name="qv_bf", align_bytes=64)
        for pair, copy in enumerate((nc.vector.tensor_copy, nc.scalar.copy)):
            qv_bank = ps.tile([P, 2, Q], F32, name="qv_bank%d" % pair)
            for e in range(2):
                t = 2 * pair + e
                nc.tensor.matmul_mx(
                    out=qv_bank[:, e, :],
                    lhsT=wq_dealt[:, t, :].bitcast(FP8X4),
                    lhsT_scale=wq_dealt_plane[:, t, :],
                    rhs=states_codes[:].bitcast(FP8X4),
                    rhs_scale=states_plane[:],
                    start=True,
                    stop=True,
                )
            copy(out=qv_bf[:, :, 2 * pair : 2 * pair + 2], in_=qv_bank[:].rearrange("p e q -> p q e"))
        qv_codes = sb.tile([P, Q], U32, name="qv_codes", align_bytes=64)
        qv_plane = sb.tile([P, Q], U8, name="qv_plane", align_bytes=64)
        nc.vector.quantize_mx(
            out=qv_codes[:].bitcast(FP8X4), scales=qv_plane[:], in_=qv_bf[:].rearrange("p q t -> p (q t)")
        )

        neg_tau = sb.tile([P, 1], F32, name="neg_tau")
        nc.vector.tensor_scalar(out=neg_tau[:], in0=tau_col[:], scalar1=-1.0, scalar2=None, op0=ALU.mult)

        scores = sb.tile([P, T], F32, name="scores", align_bytes=64)
        running = []
        for c in range(T // A_CHUNK):
            cols = slice(c * A_CHUNK, (c + 1) * A_CHUNK)
            a_bank = ps.tile([P, A_CHUNK], F32, name="a_bank%d" % c)
            nc.tensor.matmul_mx(
                out=a_bank[:],
                lhsT=qv_codes[:].bitcast(FP8X4),
                lhsT_scale=qv_plane[:],
                rhs=keys_codes[:, cols].bitcast(FP8X4),
                rhs_scale=keys_plane[:, cols],
                start=True,
                stop=True,
            )
            largest = sb.tile([P, 1], F32, name="largest%d" % c)
            nc.vector.tensor_scalar(
                out=scores[:, cols],
                in0=a_bank[:],
                scalar1=1.0,
                scalar2=running[c - 2][:] if c >= 2 else None,
                op0=ALU.mult,
                op1=ALU.max,
                accum_out=largest[:],
            )
            running.append(largest)
        neg_bt = sb.tile([P, 1], F32, name="neg_bt")
        nc.vector.tensor_scalar(
            out=neg_bt[:], in0=running[-2][:], scalar1=running[-1][:], scalar2=neg_tau[:], op0=ALU.max, op1=ALU.mult
        )

        b_banks = []
        for h in range(U // BANK):
            b_bank = ps.tile([P, BANK], F32, name="b_bank%d" % h)
            nc.tensor.matmul_mx(
                out=b_bank[:],
                lhsT=states_codes[:].bitcast(FP8X4),
                lhsT_scale=states_plane[:],
                rhs=notes_codes[:, 2 * BANK * h : 2 * BANK * (h + 1)].bitcast(FP4X4),
                rhs_scale=notes_plane[:, BANK * h : BANK * (h + 1)],
                start=True,
                stop=True,
            )
            b_banks.append(b_bank)

        e1 = sb.tile([P, SLOTS], F32, name="e1", align_bytes=64)
        for h in range(2):
            slots = slice(h * HALF, (h + 1) * HALF)
            list_cols = slice(h * HALF_COLS, (h + 1) * HALF_COLS)
            nc.scalar.activation(
                out=e1[:, slots],
                in_=scores[:].indirect(token_list[:, list_cols]),
                func=ACT.Exp,
                bias=neg_bt[:],
                scale=tau_col[:],
            )
            nc.vector.tensor_tensor(out=votes[:].indirect(vote_list[:, list_cols]), in0=e1[:, slots], in1=fours[:], op=ALU.mult)

        b_side = sb.tile([P, SIDE], F32, name="b_side", align_bytes=64)
        nc.scalar.copy(out=b_side[:], in_=b_banks[1][:, BANK - SIDE :])
        cc = sb.tile([P, U], F32, name="cc", align_bytes=64)
        split = U - SIDE
        nc.gpsimd.tensor_tensor(out=cc[:, split:], in0=votes[:, split:], in1=b_side[:], op=ALU.add)
        nc.vector.tensor_tensor(out=cc[:, :BANK], in0=votes[:, :BANK], in1=b_banks[0][:], op=ALU.add)
        nc.vector.tensor_tensor(out=cc[:, BANK:split], in0=votes[:, BANK:split], in1=b_banks[1][:, : split - BANK], op=ALU.add)

        low = sb.tile([P, HALF], F32, name="low", align_bytes=64)
        picked = sb.tile([P, HALF], F32, name="picked", align_bytes=64)
        high = sb.tile([P, HALF], F32, name="high", align_bytes=64)
        nc.vector.tensor_tensor(
            out=low[:], in0=cc[:].indirect(read_list[:, :HALF_COLS]), in1=e1[:, :HALF], op=ALU.subtract
        )
        nc.scalar.activation(out=picked[:], in_=cc[:].indirect(read_list[:, HALF_COLS:]), func=ACT.Copy)
        nc.sync.dma_start(out=out[:, :HALF], in_=low[:])
        nc.vector.tensor_tensor(out=high[:], in0=picked[:], in1=e1[:, HALF:], op=ALU.subtract)
        nc.sync.dma_start(out=out[:, HALF:], in_=high[:])
